import numpy as np
import ml_dtypes


def mxq(x, axis, fmt="e4m3"):
    dtype, down = {"e4m3": (ml_dtypes.float8_e4m3fn, 7), "e5m2": (ml_dtypes.float8_e5m2, 14)}[fmt]
    v = np.moveaxis(np.asarray(x, np.float32).astype(ml_dtypes.bfloat16).astype(np.float64), axis, -1)
    blocks = v.reshape(v.shape[:-1] + (-1, 32))
    amax = np.abs(blocks).max(-1, keepdims=True)
    byte = np.maximum(np.where(amax > 0, np.frexp(amax)[1] - 1 + 127, 0) - down, 1)
    scale = np.exp2(byte - 127.0)
    codes = (blocks / scale).astype(np.float32).astype(dtype).astype(np.float64)
    return np.moveaxis((codes * scale).reshape(v.shape), -1, axis)


WIDE = False


def mx_kscale(k):
    if not WIDE:
        return np.ones(k)
    levels = np.array([10, -10, 5, -5, 0])
    if k % 512:
        return np.exp2(np.random.permutation(np.resize(levels, k // 32))).repeat(32)
    a = np.empty((k // 512, 16))
    for p in range(k // 512):
        a[p, :8] = np.random.permutation(np.resize(levels, 8))
        for g in range(8):
            far = levels[np.abs(levels - a[p, g]) >= 10]
            a[p, g + 8] = far[np.random.randint(len(far))]
    return np.exp2(a.ravel()).repeat(32)


def f64(x):
    return np.asarray(x).astype(np.float64)


def striped(idx):
    return np.tile(idx.reshape(-1, 16).T, (8, 1)).astype(np.uint16)


def unstriped(offs):
    return offs[:16].T.reshape(-1).astype(np.int64)


E2M1 = np.array([0.0, 0.5, 1.0, 1.5, 2.0, 3.0, 4.0, 6.0, -0.0, -0.5, -1.0, -1.5, -2.0, -3.0, -4.0, -6.0])


def pack_weight(w, fmt):
    k, n = w.shape
    w = f64(np.asarray(w, np.float32).astype(ml_dtypes.bfloat16)).reshape(k // 32, 32, n)
    amax = np.abs(w).max(1)
    if fmt == "e4m3":
        byte = np.frexp(amax)[1] - 1 + 127 - 7
    else:
        mant, ex = np.frexp(amax / 6.0)
        byte = np.where(mant > 0.5, ex, ex - 1) + 127
    byte = np.clip(np.where(amax > 0, byte, 1), 1, 254)
    scaled = (w * np.exp2(127.0 - byte)[:, None, :]).reshape(k, n).astype(np.float32)
    by_word = np.ascontiguousarray(scaled.reshape(k // 512, 128, 4, n).transpose(0, 1, 3, 2))
    if fmt == "e4m3":
        words = by_word.astype(ml_dtypes.float8_e4m3fn).view(np.uint8)
    else:
        c = by_word.astype(ml_dtypes.float4_e2m1fn).view(np.uint8) & 0xF
        words = (c[..., 0::2] | (c[..., 1::2] << 4)).reshape(k // 512, 128, 2 * n)
    return np.ascontiguousarray(words), np.ascontiguousarray(byte.astype(np.uint8).reshape(k // 512, 16, n))


def unpack_weight(words, scales, fmt):
    g, _, n = scales.shape
    words = np.ascontiguousarray(words).reshape(g, 128, n, -1)
    if fmt == "e4m3":
        vals = words.view(ml_dtypes.float8_e4m3fn).astype(np.float64)
    else:
        nib = np.empty((g, 128, n, 4), np.uint8)
        nib[..., 0::2] = words & 0xF
        nib[..., 1::2] = words >> 4
        vals = E2M1[nib]
    vals = vals * np.repeat(np.exp2(scales.astype(np.float64) - 127.0), 8, axis=1)[..., None]
    return vals.transpose(0, 1, 3, 2).reshape(g * 512, n)


def gelu(v):
    return 0.5 * v * (1.0 + np.tanh(np.sqrt(2.0 / np.pi) * (v + 0.044715 * v**3)))


def striped8(idx):
    return np.concatenate([v.reshape(-1, 16).T for v in idx]).astype(np.uint16)


def unstriped8(offs):
    return np.stack([offs[16 * g:16 * g + 16].T.reshape(-1) for g in range(8)]).astype(np.int64)


def runs(v, idx8):
    k = np.arange(v.shape[0])
    return v[k[:, None], idx8[k % 512 // 64]]


def put_heads(h, wgs, idx8, t2):
    r = np.arange(h.shape[0])
    page = np.zeros((h.shape[0], t2))
    page[r[:, None], idx8[r % 512 // 64]] = wgs[r // 4 % 128] * h
    return page


K, H, N, T, S, T2 = 512, 1536, 512, 2048, 1024, 2048

def setup_inputs():
    n = np.random.standard_normal
    s = mx_kscale(K)[:, None]
    u = mx_kscale(H)[:, None]
    tab_words, tab_scales = pack_weight(n((K, T)) * s, "e4m3")
    wb_words, wb_scales = pack_weight(0.5 * n((H, N)) / np.sqrt(H) / u, "e2m1")
    return {
        "tab_words": tab_words,
        "tab_scales": tab_scales,
        "wa": (n((K, H)) / np.sqrt(K) / s).astype(np.float32),
        "cen": (0.7 * n((H, S))).astype(np.float32),
        "gain": (np.exp(0.3 * n(H)) * u[:, 0]).astype(np.float32),
        "wb_words": wb_words,
        "wb_scales": wb_scales,
        "spread": np.random.uniform(0.5, 2.0, N).astype(np.float32),
        "wgo": np.repeat(np.random.uniform(0.5, 2.0, (8, S)), 16, axis=0).astype(np.float32),
        "offs": striped8(np.stack([np.random.permutation(T)[:S] for _ in range(8)])),
        "offs2": striped8(np.stack([np.random.permutation(T2)[:S] for _ in range(8)])),
    }

def reference(tab_words, tab_scales, wa, cen, gain, wb_words, wb_scales, spread, wgo, offs, offs2):
    v = runs(unpack_weight(tab_words, tab_scales, "e4m3"), unstriped8(offs))
    d = (mxq(f64(wa), 0, "e4m3").T @ v) - f64(cen)
    h = d * d * f64(gain)[:, None]
    wb = unpack_weight(wb_words, wb_scales, "e2m1")
    y = (wb.T @ mxq(h, 0, "e4m3")) / f64(spread)[:, None]
    out = put_heads(y, f64(wgo), unstriped8(offs2), T2)
    return out

@@ -1,0 +1,240 @@
+from contextlib import ExitStack
+
+import concourse.mybir as mybir
+
+K, H, N, T, S, T2 = 512, 1536, 512, 2048, 1024, 2048
+FLOPS = 2 * K * H * S + 2 * H * N * S
+
+F32 = mybir.dt.float32
+BF16 = mybir.dt.bfloat16
+I32 = mybir.dt.int32
+U32 = mybir.dt.uint32
+U16 = mybir.dt.uint16
+U8 = mybir.dt.uint8
+FP8X4 = mybir.dt.float8_e4m3fn_x4
+FP4X4 = mybir.dt.float4_e2m1fn_x4
+ALU = mybir.AluOpType
+ACT = mybir.ActivationFunctionType
+
+P = 128
+PACK = 4
+PASS = P * PACK
+BLOCKS = H // PASS
+HALF = 512
+HALVES = S // HALF
+LIST_COLS = HALF // 16
+SHIFT = 14
+MOVED = 112
+
+
+def tile_list_codeword_migration_squares_kernel(
+    tc, tab_words, tab_scales, wa, cen, gain, wb_words, wb_scales, spread, wgo, offs, offs2, out
+):
+    nc = tc.nc
+    with ExitStack() as ctx:
+        keep = ctx.enter_context(tc.tile_pool(name="keep", bufs=1))
+        ring = ctx.enter_context(tc.tile_pool(name="ring", bufs=2))
+        psum1 = ctx.enter_context(tc.psum_pool(name="psum1", bufs=4))
+        psum2 = ctx.enter_context(tc.psum_pool(name="psum2", bufs=1))
+
+        picks = keep.tile([P, S // 16], U16, name="picks")
+        slots = keep.tile([P, S // 16], U16, name="slots")
+        tab_w = keep.tile([P, T], I32, name="tab_w", tag="slot_c", align_bytes=64)
+        tab_s = keep.tile([P, T], U8, name="tab_s", tag="slot_a", align_bytes=64)
+        gain_sb = keep.tile([P, BLOCKS, PACK], F32, name="gain_sb")
+        root = keep.tile([P, BLOCKS, PACK], F32, name="root")
+        spread_sb = keep.tile([P, PACK], F32, name="spread_sb")
+        inv_spread = keep.tile([P, PACK], F32, name="inv_spread")
+        wb_w_raw = keep.tile([P, BLOCKS, 2 * N], U8, name="wb_w_raw", tag="slot_b", align_bytes=64)
+        wb_s_raw = keep.tile([P, N], U8, name="wb_s_raw", align_bytes=64)
+        wb_w = keep.tile([P, BLOCKS, 2 * N], U8, name="wb_w", align_bytes=64)
+        wb_s = [keep.tile([P, N], U8, name=f"wb_s{a}", align_bytes=64) for a in range(BLOCKS)]
+        v_w = [keep.tile([P, HALF], I32, name=f"v_w{h}", align_bytes=64) for h in range(HALVES)]
+        v_s_picked = [keep.tile([P, HALF], U8, name=f"v_sp{h}", align_bytes=64) for h in range(HALVES)]
+        v_s = [keep.tile([P, HALF], U8, name=f"v_s{h}", align_bytes=64) for h in range(HALVES)]
+        wa_w = [keep.tile([P, PASS], U32, name=f"wa_w{b}", align_bytes=64) for b in range(BLOCKS)]
+        wa_s = [keep.tile([P, PASS], U8, name=f"wa_s{b}", align_bytes=64) for b in range(BLOCKS)]
+        pages = [keep.tile([P, T2], F32, name=f"page{i}") for i in range(PACK)]
+
+        nc.sync.dma_start(picks[:], offs)
+
+        def load_wa(b, s, pieces, tag):
+            width = PASS // pieces
+            raw = keep.tile([P, PACK, width], F32, name=f"wa_raw{b}_{s}", tag=tag, align_bytes=64)
+            c0 = PASS * b + width * s
+            nc.sync.dma_start(raw[:], wa[:, c0 : c0 + width].rearrange("(p j) c -> p j c", j=PACK))
+            return raw
+
+        scale_rows = tab_scales[0].bitcast(I32).rearrange("(g e) c -> e g c", e=2)
+        for e in range(2):
+            nc.sync.dma_start(
+                tab_s[e:P:2, :].bitcast(I32),
+                scale_rows[e].unsqueeze(1).broadcast_to([8, 8, T // 4]),
+            )
+        nc.sync.dma_start(wb_w_raw[:].bitcast(I32), wb_words.rearrange("a p c -> p a c").bitcast(I32))
+        nc.sync.dma_start(tab_w[:], tab_words[0].rearrange("p t i -> p (t i)").bitcast(I32))
+        nc.gpsimd.dma_start(gain_sb[:], gain.rearrange("(b p t) -> p b t", p=P, t=PACK))
+        nc.scalar.activation(root[:], gain_sb[:], ACT.Sqrt)
+        for h in range(HALVES):
+            nc.vector.memset(v_s[h][:].bitcast(I32), 0)
+        nc.vector.memset(wb_s_raw[:].bitcast(I32), 0)
+        for a in range(1, BLOCKS):
+            nc.vector.memset(wb_s[a][:].bitcast(I32), 0)
+
+        def gather(h):
+            cols = picks[:, h * LIST_COLS : (h + 1) * LIST_COLS]
+            nc.vector.tensor_copy(v_s_picked[h][:], tab_s[:].indirect(cols))
+            nc.scalar.dma_start(
+                v_s[h][0:MOVED, :].bitcast(I32), v_s_picked[h][SHIFT : SHIFT + MOVED, :].bitcast(I32)
+            )
+            nc.vector.tensor_copy(v_w[h][:].bitcast(U32), tab_w[:].bitcast(U32).indirect(cols))
+
+        def prepare_wa(b, raws, tag):
+            grouped = keep.tile([P, PACK, P, PACK], BF16, name=f"wa_grouped{b}", tag=tag, align_bytes=64)
+            width = PASS // len(raws)
+            for s, raw in enumerate(raws):
+                m0 = width // PACK * s
+                nc.scalar.copy(
+                    grouped[:, :, m0 : m0 + width // PACK, :].rearrange("p t m j -> p m j t"),
+                    raw[:].rearrange("p j (m t) -> p m j t", t=PACK),
+                )
+            nc.vector.quantize_mx(
+                out=wa_w[b][:].bitcast(FP8X4),
+                scales=wa_s[b][:],
+                in_=grouped[:].rearrange("p t m j -> p (t m j)"),
+            )
+
+        def load_cen(b, h, tag):
+            c = keep.tile([P, PACK, HALF], F32, name=f"cen{b}_{h}", tag=tag, align_bytes=64)
+            rows = cen[PASS * b : PASS * (b + 1), HALF * h : HALF * (h + 1)]
+            nc.sync.dma_start(c[:], rows.rearrange("(p t) j -> p t j", t=PACK))
+            return c
+
+        def offsets(b, h, c, on_gpsimd):
+            for t in range(PACK):
+                s = root[:, b, t : t + 1]
+                if on_gpsimd:
+                    nc.gpsimd.tensor_scalar(c[:, t, :], c[:, t, :], s, 0.0, ALU.mult, ALU.add)
+                else:
+                    nc.scalar.activation(c[:, t, :], c[:, t, :], ACT.Copy, scale=s)
+                acc = psum1.tile([P, HALF], F32, name="acc1")
+                m = slice(P * t, P * (t + 1))
+                nc.tensor.matmul_mx(
+                    out=acc[:],
+                    lhsT=wa_w[b][:, m].bitcast(FP8X4),
+                    lhsT_scale=wa_s[b][:, m],
+                    rhs=v_w[h][:].bitcast(FP8X4),
+                    rhs_scale=v_s[h][:],
+                    start=True,
+                    stop=True,
+                )
+                nc.vector.scalar_tensor_tensor(c[:, t, :], acc[:], s, c[:, t, :], ALU.mult, ALU.subtract)
+
+        def square(c):
+            hb = ring.tile([P, HALF, PACK], BF16, name="h_grouped", align_bytes=64, bufs=3)
+            nc.scalar.activation(
+                hb[:].rearrange("p (c i) t -> p c t i", i=4),
+                c[:].rearrange("p t (c i) -> p c t i", i=4),
+                ACT.Square,
+            )
+            return hb
+
+        def quantise(hb):
+            h_w = ring.tile([P, HALF], U32, name="h_w", align_bytes=64, bufs=6)
+            h_s = ring.tile([P, HALF], U8, name="h_s", align_bytes=64, bufs=6)
+            nc.vector.quantize_mx(
+                out=h_w[:].bitcast(FP8X4), scales=h_s[:], in_=hb[:].rearrange("p c t -> p (c t)")
+            )
+            return h_w, h_s
+
+        def second(b, hq, accs):
+            h_w, h_s = hq
+            for i in range(PACK):
+                nc.tensor.matmul_mx(
+                    out=accs[i][:],
+                    lhsT=wb_w[:, b, 2 * P * i : 2 * P * (i + 1)].bitcast(FP4X4),
+                    lhsT_scale=wb_s[b][:, P * i : P * (i + 1)],
+                    rhs=h_w[:].bitcast(FP8X4),
+                    rhs_scale=h_s[:],
+                    start=(b == 0),
+                    stop=(b == BLOCKS - 1),
+                )
+
+        def place(h, i, acc, on_vector=False):
+            y = ring.tile([P, HALF], F32, name="y", bufs=8)
+            if on_vector:
+                nc.vector.tensor_scalar(y[:], acc[:], inv_spread[:, i : i + 1], None, ALU.mult)
+            else:
+                nc.scalar.activation(y[:], acc[:], ACT.Copy, scale=inv_spread[:, i : i + 1])
+            cols = slots[:, h * LIST_COLS : (h + 1) * LIST_COLS]
+            nc.vector.tensor_tensor(pages[i][:].indirect(cols), y[:], wgo_sb[:, HALF * h : HALF * (h + 1)], ALU.mult)
+
+        gather(0)
+        nc.vector.tensor_copy(
+            wb_w[:].bitcast(U16).rearrange("p a (i m) -> p a i m", i=PACK),
+            wb_w_raw[:].bitcast(U16).rearrange("p a (m i) -> p a i m", i=PACK),
+        )
+        gather(1)
+        prepare_wa(0, [load_wa(0, 0, 2, "wa_raw0a"), load_wa(0, 1, 2, "slot_d")], "slot_e")
+        nc.sync.dma_start(slots[:], offs2)
+        for q in range(4):
+            nc.gpsimd.dma_start(
+                wb_s_raw[32 * q : 32 * q + 4 * BLOCKS, :].bitcast(I32),
+                wb_scales[:, 4 * q : 4 * q + 4, :].bitcast(I32),
+            )
+        nc.gpsimd.dma_start(spread_sb[:], spread.rearrange("(p i) -> p i", i=PACK))
+        c00 = load_cen(0, 0, "slot_a")
+        prepare_wa(1, [load_wa(1, 0, 1, "slot_b")], "slot_f")
+        c01 = load_cen(0, 1, "slot_c")
+        c10 = load_cen(1, 0, "slot_d")
+        wa2 = load_wa(2, 0, 1, "slot_e")
+        c11 = load_cen(1, 1, "slot_b")
+        c20 = load_cen(2, 0, "slot_f")
+
+        nc.vector.tensor_copy(
+            wb_s[0][:].rearrange("p (i m) -> p i m", i=PACK),
+            wb_s_raw[:].rearrange("p (m i) -> p i m", i=PACK),
+        )
+        for a in range(1, BLOCKS):
+            nc.gpsimd.dma_start(
+                wb_s[a][0:MOVED, :].bitcast(I32), wb_s[0][4 * a : 4 * a + MOVED, :].bitcast(I32)
+            )
+        nc.vector.reciprocal(inv_spread[:], spread_sb[:])
+
+        acc0 = [psum2.tile([P, HALF], F32, name=f"acc2_{i}") for i in range(PACK)]
+        offsets(0, 0, c00, True)
+        h00 = square(c00)
+        c21 = load_cen(2, 1, "slot_a")
+        offsets(0, 1, c01, True)
+        second(0, quantise(h00), acc0)
+        h01 = square(c01)
+        prepare_wa(2, [wa2], "slot_c")
+        wgo_sb = keep.tile([P, S], F32, name="wgo_sb", tag="slot_e", align_bytes=64)
+        nc.sync.dma_start(wgo_sb[:], wgo)
+        offsets(1, 0, c10, True)
+        q01 = quantise(h01)
+        h10 = square(c10)
+        offsets(1, 1, c11, True)
+        second(1, quantise(h10), acc0)
+        h11 = square(c11)
+        offsets(2, 0, c20, True)
+        h20 = square(c20)
+        offsets(2, 1, c21, True)
+        q11 = quantise(h11)
+        second(2, quantise(h20), acc0)
+        h21 = square(c21)
+        for i in range(PACK):
+            eng = nc.vector if i < 3 else nc.gpsimd
+            eng.memset(pages[i][:], 0.0)
+        place(0, 0, acc0[0], True)
+        q21 = quantise(h21)
+        acc1 = [psum1.tile([P, HALF], F32, name="acc1") for i in range(PACK)]
+        second(0, q01, acc1)
+        second(1, q11, acc1)
+        second(2, q21, acc1)
+        for i in range(1, PACK):
+            place(0, i, acc0[i])
+        rows = out.rearrange("(p i) t -> p i t", i=PACK)
+        for i in range(PACK):
+            place(1, i, acc1[i])
+            nc.sync.dma_start(rows[:, i, :], pages[i][:])

@@ -46,15 +46,15 @@ def tile_list_codeword_migration_squares_kernel(
         spread_sb = keep.tile([P, PACK], F32, name="spread_sb")
         inv_spread = keep.tile([P, PACK], F32, name="inv_spread")
         wb_w_raw = keep.tile([P, BLOCKS, 2 * N], U8, name="wb_w_raw", tag="slot_b", align_bytes=64)
-        wb_s_raw = keep.tile([P, N], U8, name="wb_s_raw", align_bytes=64)
+        wb_s_raw = keep.tile([P, N], U8, name="wb_s_raw", tag="slot_h", align_bytes=64)
         wb_w = keep.tile([P, BLOCKS, 2 * N], U8, name="wb_w", align_bytes=64)
-        wb_s = [keep.tile([P, N], U8, name=f"wb_s{a}", align_bytes=64) for a in range(BLOCKS)]
+        wb_s = {a: keep.tile([P, N], U8, name=f"wb_s{a}", align_bytes=64) for a in range(1, BLOCKS)}
         v_w = [keep.tile([P, HALF], I32, name=f"v_w{h}", align_bytes=64) for h in range(HALVES)]
-        v_s_picked = [keep.tile([P, HALF], U8, name=f"v_sp{h}", align_bytes=64) for h in range(HALVES)]
-        v_s = [keep.tile([P, HALF], U8, name=f"v_s{h}", align_bytes=64) for h in range(HALVES)]
+        v_s_picked = keep.tile([P, S], U8, name="v_s_picked", align_bytes=64)
+        v_s = keep.tile([P, S], U8, name="v_s", align_bytes=64)
         wa_w = [keep.tile([P, PASS], U32, name=f"wa_w{b}", align_bytes=64) for b in range(BLOCKS)]
         wa_s = [keep.tile([P, PASS], U8, name=f"wa_s{b}", align_bytes=64) for b in range(BLOCKS)]
-        pages = [keep.tile([P, T2], F32, name=f"page{i}") for i in range(PACK)]
+        pages = [keep.tile([P, T2], F32, name=f"page{i}") for i in range(2)]
 
         nc.sync.dma_start(picks[:], offs)
 
@@ -74,19 +74,15 @@ def tile_list_codeword_migration_squares_kernel(
         nc.sync.dma_start(wb_w_raw[:].bitcast(I32), wb_words.rearrange("a p c -> p a c").bitcast(I32))
         nc.sync.dma_start(tab_w[:], tab_words[0].rearrange("p t i -> p (t i)").bitcast(I32))
         nc.gpsimd.dma_start(gain_sb[:], gain.rearrange("(b p t) -> p b t", p=P, t=PACK))
+        nc.gpsimd.dma_start(spread_sb[:], spread.rearrange("(p i) -> p i", i=PACK))
         nc.scalar.activation(root[:], gain_sb[:], ACT.Sqrt)
-        for h in range(HALVES):
-            nc.vector.memset(v_s[h][:].bitcast(I32), 0)
+        nc.vector.memset(v_s[:].bitcast(I32), 0)
         nc.vector.memset(wb_s_raw[:].bitcast(I32), 0)
         for a in range(1, BLOCKS):
             nc.vector.memset(wb_s[a][:].bitcast(I32), 0)
 
         def gather(h):
             cols = picks[:, h * LIST_COLS : (h + 1) * LIST_COLS]
-            nc.vector.tensor_copy(v_s_picked[h][:], tab_s[:].indirect(cols))
-            nc.scalar.dma_start(
-                v_s[h][0:MOVED, :].bitcast(I32), v_s_picked[h][SHIFT : SHIFT + MOVED, :].bitcast(I32)
-            )
             nc.vector.tensor_copy(v_w[h][:].bitcast(U32), tab_w[:].bitcast(U32).indirect(cols))
 
         def prepare_wa(b, raws, tag):
@@ -104,58 +100,71 @@ def tile_list_codeword_migration_squares_kernel(
                 in_=grouped[:].rearrange("p t m j -> p (t m j)"),
             )
 
-        def load_cen(b, h, tag):
-            c = keep.tile([P, PACK, HALF], F32, name=f"cen{b}_{h}", tag=tag, align_bytes=64)
-            rows = cen[PASS * b : PASS * (b + 1), HALF * h : HALF * (h + 1)]
-            nc.sync.dma_start(c[:], rows.rearrange("(p t) j -> p t j", t=PACK))
+        def slot(shape, dtype, name, tag):
+            return keep.tile(shape, dtype, name=name, tag=tag, align_bytes=64)
+
+        def load_cen_pairs(b, tag):
+            c = slot([P, PACK, S], F32, f"cen{b}", tag)
+            rows = cen[PASS * b : PASS * (b + 1), :].rearrange("(p t) j -> p t j", t=PACK)
+            for t0 in (0, 2):
+                nc.sync.dma_start(c[:, t0 : t0 + 2, :], rows[:, t0 : t0 + 2, :])
             return c
 
-        def offsets(b, h, c, on_gpsimd):
-            for t in range(PACK):
-                s = root[:, b, t : t + 1]
-                if on_gpsimd:
-                    nc.gpsimd.tensor_scalar(c[:, t, :], c[:, t, :], s, 0.0, ALU.mult, ALU.add)
-                else:
-                    nc.scalar.activation(c[:, t, :], c[:, t, :], ACT.Copy, scale=s)
-                acc = psum1.tile([P, HALF], F32, name="acc1")
-                m = slice(P * t, P * (t + 1))
-                nc.tensor.matmul_mx(
-                    out=acc[:],
-                    lhsT=wa_w[b][:, m].bitcast(FP8X4),
-                    lhsT_scale=wa_s[b][:, m],
-                    rhs=v_w[h][:].bitcast(FP8X4),
-                    rhs_scale=v_s[h][:],
-                    start=True,
-                    stop=True,
-                )
-                nc.vector.scalar_tensor_tensor(c[:, t, :], acc[:], s, c[:, t, :], ALU.mult, ALU.subtract)
+        def load_cen_halves(b, tag):
+            c = slot([P, HALVES, PACK, HALF], F32, f"cen{b}", tag)
+            rows = cen[PASS * b : PASS * (b + 1), :].rearrange("(p t) j -> p t j", t=PACK)
+            for h in range(HALVES):
+                nc.sync.dma_start(c[:, h, :, :], rows[:, :, HALF * h : HALF * (h + 1)])
+            return c
 
-        def square(c):
-            hb = ring.tile([P, HALF, PACK], BF16, name="h_grouped", align_bytes=64, bufs=3)
+        def prescale(b, t, dst, src, on_scalar=False):
+            s = root[:, b, t : t + 1]
+            if on_scalar:
+                nc.scalar.activation(dst, src, ACT.Copy, scale=s)
+            else:
+                nc.gpsimd.tensor_scalar(dst, src, s, 0.0, ALU.mult, ALU.add)
+
+        def offset(b, t, h, d):
+            acc = psum1.tile([P, HALF], F32, name="acc1")
+            m = slice(P * t, P * (t + 1))
+            nc.tensor.matmul_mx(
+                out=acc[:],
+                lhsT=wa_w[b][:, m].bitcast(FP8X4),
+                lhsT_scale=wa_s[b][:, m],
+                rhs=v_w[h][:].bitcast(FP8X4),
+                rhs_scale=v_s[:, HALF * h : HALF * (h + 1)],
+                start=True,
+                stop=True,
+            )
+            nc.vector.scalar_tensor_tensor(d, acc[:], root[:, b, t : t + 1], d, ALU.mult, ALU.subtract)
+
+        def offsets_pairs(b, d):
+            for t, h in ((0, 0), (0, 1), (1, 0), (1, 1), (2, 0), (3, 0), (2, 1), (3, 1)):
+                offset(b, t, h, d[:, t, HALF * h : HALF * (h + 1)])
+
+        def square(hb, d):
             nc.scalar.activation(
-                hb[:].rearrange("p (c i) t -> p c t i", i=4),
-                c[:].rearrange("p t (c i) -> p c t i", i=4),
+                hb.rearrange("p (c i) t -> p c t i", i=4),
+                d.rearrange("p t (c i) -> p c t i", i=4),
                 ACT.Square,
             )
-            return hb
 
-        def quantise(hb):
-            h_w = ring.tile([P, HALF], U32, name="h_w", align_bytes=64, bufs=6)
-            h_s = ring.tile([P, HALF], U8, name="h_s", align_bytes=64, bufs=6)
+        def quantise(hb, width, name, tag):
+            h_w = slot([P, width], U32, name + "_w", tag)
+            h_s = slot([P, width], U8, name + "_s", name + "_s")
             nc.vector.quantize_mx(
                 out=h_w[:].bitcast(FP8X4), scales=h_s[:], in_=hb[:].rearrange("p c t -> p (c t)")
             )
             return h_w, h_s
 
-        def second(b, hq, accs):
-            h_w, h_s = hq
-            for i in range(PACK):
+        def second(i, acc, operands):
+            for b, (h_w, h_s) in enumerate(operands):
                 nc.tensor.matmul_mx(
-                    out=accs[i][:],
+                    out=acc[:],
                     lhsT=wb_w[:, b, 2 * P * i : 2 * P * (i + 1)].bitcast(FP4X4),
                     lhsT_scale=wb_s[b][:, P * i : P * (i + 1)],
-                    rhs=h_w[:].bitcast(FP8X4),
-                    rhs_scale=h_s[:],
+                    rhs=h_w.bitcast(FP8X4),
+                    rhs_scale=h_s,
                     start=(b == 0),
                     stop=(b == BLOCKS - 1),
                 )
@@ -167,30 +176,31 @@ def tile_list_codeword_migration_squares_kernel(
             else:
                 nc.scalar.activation(y[:], acc[:], ACT.Copy, scale=inv_spread[:, i : i + 1])
             cols = slots[:, h * LIST_COLS : (h + 1) * LIST_COLS]
-            nc.vector.tensor_tensor(pages[i][:].indirect(cols), y[:], wgo_sb[:, HALF * h : HALF * (h + 1)], ALU.mult)
+            nc.vector.tensor_tensor(
+                pages[i][:].indirect(cols), y[:], wgo_sb[:, HALF * h : HALF * (h + 1)], ALU.mult
+            )
 
-        gather(0)
+        nc.vector.tensor_copy(v_s_picked[:], tab_s[:].indirect(picks[:]))
+        nc.scalar.dma_start(v_s[0:MOVED, :].bitcast(I32), v_s_picked[SHIFT : SHIFT + MOVED, :].bitcast(I32))
         nc.vector.tensor_copy(
             wb_w[:].bitcast(U16).rearrange("p a (i m) -> p a i m", i=PACK),
             wb_w_raw[:].bitcast(U16).rearrange("p a (m i) -> p a i m", i=PACK),
         )
+        nc.vector.reciprocal(inv_spread[:], spread_sb[:])
+        gather(0)
         gather(1)
-        prepare_wa(0, [load_wa(0, 0, 2, "wa_raw0a"), load_wa(0, 1, 2, "slot_d")], "slot_e")
+        prepare_wa(0, [load_wa(0, 0, 2, "slot_g"), load_wa(0, 1, 2, "slot_d")], "slot_e")
         nc.sync.dma_start(slots[:], offs2)
         for q in range(4):
             nc.gpsimd.dma_start(
                 wb_s_raw[32 * q : 32 * q + 4 * BLOCKS, :].bitcast(I32),
                 wb_scales[:, 4 * q : 4 * q + 4, :].bitcast(I32),
             )
-        nc.gpsimd.dma_start(spread_sb[:], spread.rearrange("(p i) -> p i", i=PACK))
-        c00 = load_cen(0, 0, "slot_a")
-        prepare_wa(1, [load_wa(1, 0, 1, "slot_b")], "slot_f")
-        c01 = load_cen(0, 1, "slot_c")
-        c10 = load_cen(1, 0, "slot_d")
-        wa2 = load_wa(2, 0, 1, "slot_e")
-        c11 = load_cen(1, 1, "slot_b")
-        c20 = load_cen(2, 0, "slot_f")
+        c0 = load_cen_pairs(0, "slot_b")
+        prepare_wa(1, [load_wa(1, 0, 2, "slot_c"), load_wa(1, 1, 2, "slot_g")], "slot_f")
+        c1 = load_cen_pairs(1, "slot_d")
 
+        wb_s[0] = slot([P, N], U8, "wb_s0", "slot_e")
         nc.vector.tensor_copy(
             wb_s[0][:].rearrange("p (i m) -> p i m", i=PACK),
             wb_s_raw[:].rearrange("p (m i) -> p i m", i=PACK),
@@ -199,41 +209,63 @@ def tile_list_codeword_migration_squares_kernel(
             nc.gpsimd.dma_start(
                 wb_s[a][0:MOVED, :].bitcast(I32), wb_s[0][4 * a : 4 * a + MOVED, :].bitcast(I32)
             )
-        nc.vector.reciprocal(inv_spread[:], spread_sb[:])
+        wa2 = load_wa(2, 0, 1, "slot_h")
+        c2 = load_cen_halves(2, "slot_c")
 
-        acc0 = [psum2.tile([P, HALF], F32, name=f"acc2_{i}") for i in range(PACK)]
-        offsets(0, 0, c00, True)
-        h00 = square(c00)
-        c21 = load_cen(2, 1, "slot_a")
-        offsets(0, 1, c01, True)
-        second(0, quantise(h00), acc0)
-        h01 = square(c01)
-        prepare_wa(2, [wa2], "slot_c")
-        wgo_sb = keep.tile([P, S], F32, name="wgo_sb", tag="slot_e", align_bytes=64)
+        for t in range(PACK):
+            prescale(0, t, c0[:, t, :], c0[:, t, :], on_scalar=t < 2)
+        offsets_pairs(0, c0)
+        hb0 = slot([P, S, PACK], BF16, "hb0", "slot_g")
+        for h in range(HALVES):
+            cols = slice(HALF * h, HALF * (h + 1))
+            square(hb0[:, cols, :], c0[:, :, cols])
+        d1 = slot([P, PACK, S], F32, "d1", "slot_f")
+        for h in range(HALVES):
+            cols = slice(HALF * h, HALF * (h + 1))
+            prescale(1, 0, d1[:, 0, cols], c1[:, 0, cols])
+        for t in range(1, PACK):
+            prescale(1, t, d1[:, t, :], c1[:, t, :])
+        offsets_pairs(1, d1)
+        prepare_wa(2, [wa2], "slot_b")
+        wgo_sb = slot([P, S], F32, "wgo_sb", "slot_h")
         nc.sync.dma_start(wgo_sb[:], wgo)
-        offsets(1, 0, c10, True)
-        q01 = quantise(h01)
-        h10 = square(c10)
-        offsets(1, 1, c11, True)
-        second(1, quantise(h10), acc0)
-        h11 = square(c11)
-        offsets(2, 0, c20, True)
-        h20 = square(c20)
-        offsets(2, 1, c21, True)
-        q11 = quantise(h11)
-        second(2, quantise(h20), acc0)
-        h21 = square(c21)
+        q0 = quantise(hb0, S, "q0", "slot_d")
+        hb10 = slot([P, HALF, PACK], BF16, "hb10", "hb10")
+        square(hb10[:], d1[:, :, 0:HALF])
+        d2 = slot([P, HALVES, PACK, HALF], F32, "d2", "slot_b")
+        hb2 = [slot([P, HALF, PACK], BF16, f"hb2{h}", f"slot_page{2 + h}") for h in range(HALVES)]
+        for h in range(HALVES):
+            for t in range(PACK):
+                prescale(2, t, d2[:, h, t, :], c2[:, h, t, :], on_scalar=(h == 1 and t < 2))
+                offset(2, t, h, d2[:, h, t, :])
+            square(hb2[h][:], d2[:, h, :, :])
+        q10 = quantise(hb10, HALF, "q10", "slot_c")
+
+        def operands(h, q1, q2):
+            cols = slice(HALF * h, HALF * (h + 1))
+            return [(q0[0][:, cols], q0[1][:, cols]), (q1[0][:], q1[1][:]), (q2[0][:], q2[1][:])]
+
+        q20 = quantise(hb2[0], HALF, "q20", "q20")
+        acc0 = [psum2.tile([P, HALF], F32, name=f"acc2_{i}") for i in range(PACK)]
         for i in range(PACK):
-            eng = nc.vector if i < 3 else nc.gpsimd
-            eng.memset(pages[i][:], 0.0)
+            second(i, acc0[i], operands(0, q10, q20))
+        for i in range(2):
+            nc.vector.memset(pages[i][:], 0.0)
         place(0, 0, acc0[0], True)
-        q21 = quantise(h21)
-        acc1 = [psum1.tile([P, HALF], F32, name="acc1") for i in range(PACK)]
-        second(0, q01, acc1)
-        second(1, q11, acc1)
-        second(2, q21, acc1)
-        for i in range(1, PACK):
+        q21 = quantise(hb2[1], HALF, "q21", "q21")
+        pages.append(slot([P, T2], F32, "page2", "slot_page2"))
+        nc.gpsimd.memset(pages[2][:], 0.0)
+        place(0, 1, acc0[1])
+        hb11 = slot([P, HALF, PACK], BF16, "hb11", "slot_b")
+        square(hb11[:], d1[:, :, HALF:S])
+        q11 = quantise(hb11, HALF, "q11", "q11")
+        pages.append(slot([P, T2], F32, "page3", "slot_b"))
+        nc.gpsimd.memset(pages[3][:], 0.0)
+        for i in range(2, PACK):
             place(0, i, acc0[i])
+        acc1 = [psum1.tile([P, HALF], F32, name="acc1") for i in range(PACK)]
+        for i in range(PACK):
+            second(i, acc1[i], operands(1, q11, q21))
         rows = out.rearrange("(p i) t -> p i t", i=PACK)
         for i in range(PACK):
             place(1, i, acc1[i])

@@ -50,7 +50,7 @@ def tile_list_codeword_migration_squares_kernel(
         wb_w = keep.tile([P, BLOCKS, 2 * N], U8, name="wb_w", align_bytes=64)
         wb_s = {a: keep.tile([P, N], U8, name=f"wb_s{a}", align_bytes=64) for a in range(1, BLOCKS)}
         v_w = [keep.tile([P, HALF], I32, name=f"v_w{h}", align_bytes=64) for h in range(HALVES)]
-        v_s_picked = keep.tile([P, S], U8, name="v_s_picked", align_bytes=64)
+        v_s_picked = keep.tile([P, S], U8, name="v_s_picked", tag="slot_g", align_bytes=64)
         v_s = keep.tile([P, S], U8, name="v_s", align_bytes=64)
         wa_w = [keep.tile([P, PASS], U32, name=f"wa_w{b}", align_bytes=64) for b in range(BLOCKS)]
         wa_s = [keep.tile([P, PASS], U8, name=f"wa_s{b}", align_bytes=64) for b in range(BLOCKS)]
@@ -124,6 +124,13 @@ def tile_list_codeword_migration_squares_kernel(
             else:
                 nc.gpsimd.tensor_scalar(dst, src, s, 0.0, ALU.mult, ALU.add)
 
+        def prescale_pairs(b, dst, src):
+            for h in range(HALVES):
+                cols = slice(HALF * h, HALF * (h + 1))
+                prescale(b, 0, dst[:, 0, cols], src[:, 0, cols])
+            for t in range(1, PACK):
+                prescale(b, t, dst[:, t, :], src[:, t, :])
+
         def offset(b, t, h, d):
             acc = psum1.tile([P, HALF], F32, name="acc1")
             m = slice(P * t, P * (t + 1))
@@ -163,8 +170,8 @@ def tile_list_codeword_migration_squares_kernel(
                     out=acc[:],
                     lhsT=wb_w[:, b, 2 * P * i : 2 * P * (i + 1)].bitcast(FP4X4),
                     lhsT_scale=wb_s[b][:, P * i : P * (i + 1)],
-                    rhs=h_w.bitcast(FP8X4),
-                    rhs_scale=h_s,
+                    rhs=h_w[:].bitcast(FP8X4),
+                    rhs_scale=h_s[:],
                     start=(b == 0),
                     stop=(b == BLOCKS - 1),
                 )
@@ -189,7 +196,7 @@ def tile_list_codeword_migration_squares_kernel(
         nc.vector.reciprocal(inv_spread[:], spread_sb[:])
         gather(0)
         gather(1)
-        prepare_wa(0, [load_wa(0, 0, 2, "slot_g"), load_wa(0, 1, 2, "slot_d")], "slot_e")
+        prepare_wa(0, [load_wa(0, 0, 2, "wa_raw0a"), load_wa(0, 1, 2, "wa_raw0b")], "slot_e")
         nc.sync.dma_start(slots[:], offs2)
         for q in range(4):
             nc.gpsimd.dma_start(
@@ -197,8 +204,7 @@ def tile_list_codeword_migration_squares_kernel(
                 wb_scales[:, 4 * q : 4 * q + 4, :].bitcast(I32),
             )
         c0 = load_cen_pairs(0, "slot_b")
-        prepare_wa(1, [load_wa(1, 0, 2, "slot_c"), load_wa(1, 1, 2, "slot_g")], "slot_f")
-        c1 = load_cen_pairs(1, "slot_d")
+        wa1 = [load_wa(1, 0, 2, "slot_c"), load_wa(1, 1, 2, "slot_g")]
 
         wb_s[0] = slot([P, N], U8, "wb_s0", "slot_e")
         nc.vector.tensor_copy(
@@ -206,66 +212,63 @@ def tile_list_codeword_migration_squares_kernel(
             wb_s_raw[:].rearrange("p (m i) -> p i m", i=PACK),
         )
         for a in range(1, BLOCKS):
-            nc.gpsimd.dma_start(
+            nc.sync.dma_start(
                 wb_s[a][0:MOVED, :].bitcast(I32), wb_s[0][4 * a : 4 * a + MOVED, :].bitcast(I32)
             )
-        wa2 = load_wa(2, 0, 1, "slot_h")
-        c2 = load_cen_halves(2, "slot_c")
+        c1 = load_cen_pairs(1, "slot_h")
+        wa2 = load_wa(2, 0, 1, "slot_c")
+        c2 = load_cen_halves(2, "slot_g")
 
         for t in range(PACK):
-            prescale(0, t, c0[:, t, :], c0[:, t, :], on_scalar=t < 2)
+            prescale(0, t, c0[:, t, :], c0[:, t, :], on_scalar=(t % 2 == 0))
         offsets_pairs(0, c0)
-        hb0 = slot([P, S, PACK], BF16, "hb0", "slot_g")
-        for h in range(HALVES):
-            cols = slice(HALF * h, HALF * (h + 1))
-            square(hb0[:, cols, :], c0[:, :, cols])
-        d1 = slot([P, PACK, S], F32, "d1", "slot_f")
-        for h in range(HALVES):
-            cols = slice(HALF * h, HALF * (h + 1))
-            prescale(1, 0, d1[:, 0, cols], c1[:, 0, cols])
-        for t in range(1, PACK):
-            prescale(1, t, d1[:, t, :], c1[:, t, :])
+        prepare_wa(1, wa1, "wa_grouped1")
+        hb00 = slot([P, HALF, PACK], BF16, "hb00", "hb00")
+        square(hb00[:], c0[:, :, 0:HALF])
+        d1 = c1
+        prescale_pairs(1, d1, c1)
+        q00 = quantise(hb00, HALF, "q00", "q00")
         offsets_pairs(1, d1)
-        prepare_wa(2, [wa2], "slot_b")
-        wgo_sb = slot([P, S], F32, "wgo_sb", "slot_h")
+        prepare_wa(2, [wa2], "hb00")
+        wgo_sb = slot([P, S], F32, "wgo_sb", "slot_c")
         nc.sync.dma_start(wgo_sb[:], wgo)
-        q0 = quantise(hb0, S, "q0", "slot_d")
         hb10 = slot([P, HALF, PACK], BF16, "hb10", "hb10")
         square(hb10[:], d1[:, :, 0:HALF])
-        d2 = slot([P, HALVES, PACK, HALF], F32, "d2", "slot_b")
+        d2 = [c2[:, h, :, :] for h in range(HALVES)]
         hb2 = [slot([P, HALF, PACK], BF16, f"hb2{h}", f"slot_page{2 + h}") for h in range(HALVES)]
-        for h in range(HALVES):
-            for t in range(PACK):
-                prescale(2, t, d2[:, h, t, :], c2[:, h, t, :], on_scalar=(h == 1 and t < 2))
-                offset(2, t, h, d2[:, h, t, :])
-            square(hb2[h][:], d2[:, h, :, :])
-        q10 = quantise(hb10, HALF, "q10", "slot_c")
-
-        def operands(h, q1, q2):
-            cols = slice(HALF * h, HALF * (h + 1))
-            return [(q0[0][:, cols], q0[1][:, cols]), (q1[0][:], q1[1][:]), (q2[0][:], q2[1][:])]
-
+        steps = [(h, t) for h in range(HALVES) for t in range(PACK)]
+        for h, t in steps:
+            prescale(2, t, d2[h][:, t, :], c2[:, h, t, :])
+        for h, t in steps[:PACK]:
+            offset(2, t, h, d2[h][:, t, :])
+        square(hb2[0][:], d2[0])
+        for h, t in steps[PACK:-1]:
+            offset(2, t, h, d2[h][:, t, :])
+        q10 = quantise(hb10, HALF, "q10", "q10")
         q20 = quantise(hb2[0], HALF, "q20", "q20")
         acc0 = [psum2.tile([P, HALF], F32, name=f"acc2_{i}") for i in range(PACK)]
         for i in range(PACK):
-            second(i, acc0[i], operands(0, q10, q20))
+            second(i, acc0[i], (q00, q10, q20))
+        offset(2, PACK - 1, 1, d2[1][:, PACK - 1, :])
         for i in range(2):
             nc.vector.memset(pages[i][:], 0.0)
-        place(0, 0, acc0[0], True)
+        place(0, 0, acc0[0])
+        square(hb2[1][:], d2[1])
         q21 = quantise(hb2[1], HALF, "q21", "q21")
-        pages.append(slot([P, T2], F32, "page2", "slot_page2"))
-        nc.gpsimd.memset(pages[2][:], 0.0)
-        place(0, 1, acc0[1])
-        hb11 = slot([P, HALF, PACK], BF16, "hb11", "slot_b")
-        square(hb11[:], d1[:, :, HALF:S])
-        q11 = quantise(hb11, HALF, "q11", "q11")
-        pages.append(slot([P, T2], F32, "page3", "slot_b"))
-        nc.gpsimd.memset(pages[3][:], 0.0)
         for i in range(2, PACK):
-            place(0, i, acc0[i])
+            pages.append(slot([P, T2], F32, f"page{i}", f"slot_page{i}"))
+            nc.gpsimd.memset(pages[i][:], 0.0)
+        place(0, 1, acc0[1])
+        late = slot([P, HALVES, HALF, PACK], BF16, "hb_late", "slot_g")
+        square(late[:, 0, :, :], c0[:, :, HALF:S])
+        q01 = quantise(late[:, 0, :, :], HALF, "q01", "q01")
+        place(0, 2, acc0[2])
+        square(late[:, 1, :, :], d1[:, :, HALF:S])
+        q11 = quantise(late[:, 1, :, :], HALF, "q11", "q11")
+        place(0, 3, acc0[3])
         acc1 = [psum1.tile([P, HALF], F32, name="acc1") for i in range(PACK)]
         for i in range(PACK):
-            second(i, acc1[i], operands(1, q11, q21))
+            second(i, acc1[i], (q01, q11, q21))
         rows = out.rearrange("(p i) t -> p i t", i=PACK)
         for i in range(PACK):
             place(1, i, acc1[i])

from contextlib import ExitStack

import concourse.mybir as mybir

K, H, N, T, S, T2 = 512, 1536, 512, 2048, 1024, 2048
FLOPS = 2 * K * H * S + 2 * H * N * S

F32 = mybir.dt.float32
BF16 = mybir.dt.bfloat16
I32 = mybir.dt.int32
U32 = mybir.dt.uint32
U16 = mybir.dt.uint16
U8 = mybir.dt.uint8
FP8X4 = mybir.dt.float8_e4m3fn_x4
FP4X4 = mybir.dt.float4_e2m1fn_x4
ALU = mybir.AluOpType
ACT = mybir.ActivationFunctionType

P = 128
PACK = 4
PASS = P * PACK
BLOCKS = H // PASS
HALF = 512
HALVES = S // HALF
LIST_COLS = HALF // 16
SHIFT = 14
MOVED = 112


def tile_list_codeword_migration_squares_kernel(
    tc, tab_words, tab_scales, wa, cen, gain, wb_words, wb_scales, spread, wgo, offs, offs2, out
):
    nc = tc.nc
    with ExitStack() as ctx:
        keep = ctx.enter_context(tc.tile_pool(name="keep", bufs=1))
        ring = ctx.enter_context(tc.tile_pool(name="ring", bufs=2))
        psum1 = ctx.enter_context(tc.psum_pool(name="psum1", bufs=4))
        psum2 = ctx.enter_context(tc.psum_pool(name="psum2", bufs=1))

        picks = keep.tile([P, S // 16], U16, name="picks")
        slots = keep.tile([P, S // 16], U16, name="slots")
        tab_w = keep.tile([P, T], I32, name="tab_w", tag="slot_c", align_bytes=64)
        tab_s = keep.tile([P, T], U8, name="tab_s", tag="slot_a", align_bytes=64)
        gain_sb = keep.tile([P, BLOCKS, PACK], F32, name="gain_sb")
        root = keep.tile([P, BLOCKS, PACK], F32, name="root")
        spread_sb = keep.tile([P, PACK], F32, name="spread_sb")
        inv_spread = keep.tile([P, PACK], F32, name="inv_spread")
        wb_w_raw = keep.tile([P, BLOCKS, 2 * N], U8, name="wb_w_raw", tag="slot_b", align_bytes=64)
        wb_s_raw = keep.tile([P, N], U8, name="wb_s_raw", tag="slot_h", align_bytes=64)
        wb_w = keep.tile([P, BLOCKS, 2 * N], U8, name="wb_w", align_bytes=64)
        wb_s = {a: keep.tile([P, N], U8, name=f"wb_s{a}", align_bytes=64) for a in range(1, BLOCKS)}
        v_w = [keep.tile([P, HALF], I32, name=f"v_w{h}", align_bytes=64) for h in range(HALVES)]
        v_s_picked = keep.tile([P, S], U8, name="v_s_picked", tag="slot_g", align_bytes=64)
        v_s = keep.tile([P, S], U8, name="v_s", align_bytes=64)
        wa_w = [keep.tile([P, PASS], U32, name=f"wa_w{b}", align_bytes=64) for b in range(BLOCKS)]
        wa_s = [keep.tile([P, PASS], U8, name=f"wa_s{b}", align_bytes=64) for b in range(BLOCKS)]
        pages = [keep.tile([P, T2], F32, name=f"page{i}") for i in range(2)]

        nc.sync.dma_start(picks[:], offs)

        def load_wa(b, s, pieces, tag):
            width = PASS // pieces
            raw = keep.tile([P, PACK, width], F32, name=f"wa_raw{b}_{s}", tag=tag, align_bytes=64)
            c0 = PASS * b + width * s
            nc.sync.dma_start(raw[:], wa[:, c0 : c0 + width].rearrange("(p j) c -> p j c", j=PACK))
            return raw

        scale_rows = tab_scales[0].bitcast(I32).rearrange("(g e) c -> e g c", e=2)
        for e in range(2):
            nc.sync.dma_start(
                tab_s[e:P:2, :].bitcast(I32),
                scale_rows[e].unsqueeze(1).broadcast_to([8, 8, T // 4]),
            )
        nc.sync.dma_start(wb_w_raw[:].bitcast(I32), wb_words.rearrange("a p c -> p a c").bitcast(I32))
        nc.sync.dma_start(tab_w[:], tab_words[0].rearrange("p t i -> p (t i)").bitcast(I32))
        nc.gpsimd.dma_start(gain_sb[:], gain.rearrange("(b p t) -> p b t", p=P, t=PACK))
        nc.gpsimd.dma_start(spread_sb[:], spread.rearrange("(p i) -> p i", i=PACK))
        nc.scalar.activation(root[:], gain_sb[:], ACT.Sqrt)
        nc.vector.memset(v_s[:].bitcast(I32), 0)
        nc.vector.memset(wb_s_raw[:].bitcast(I32), 0)
        for a in range(1, BLOCKS):
            nc.vector.memset(wb_s[a][:].bitcast(I32), 0)

        def gather(h):
            cols = picks[:, h * LIST_COLS : (h + 1) * LIST_COLS]
            nc.vector.tensor_copy(v_w[h][:].bitcast(U32), tab_w[:].bitcast(U32).indirect(cols))

        def prepare_wa(b, raws, tag):
            grouped = keep.tile([P, PACK, P, PACK], BF16, name=f"wa_grouped{b}", tag=tag, align_bytes=64)
            width = PASS // len(raws)
            for s, raw in enumerate(raws):
                m0 = width // PACK * s
                nc.scalar.copy(
                    grouped[:, :, m0 : m0 + width // PACK, :].rearrange("p t m j -> p m j t"),
                    raw[:].rearrange("p j (m t) -> p m j t", t=PACK),
                )
            nc.vector.quantize_mx(
                out=wa_w[b][:].bitcast(FP8X4),
                scales=wa_s[b][:],
                in_=grouped[:].rearrange("p t m j -> p (t m j)"),
            )

        def slot(shape, dtype, name, tag):
            return keep.tile(shape, dtype, name=name, tag=tag, align_bytes=64)

        def load_cen_pairs(b, tag):
            c = slot([P, PACK, S], F32, f"cen{b}", tag)
            rows = cen[PASS * b : PASS * (b + 1), :].rearrange("(p t) j -> p t j", t=PACK)
            for t0 in (0, 2):
                nc.sync.dma_start(c[:, t0 : t0 + 2, :], rows[:, t0 : t0 + 2, :])
            return c

        def load_cen_halves(b, tag):
            c = slot([P, HALVES, PACK, HALF], F32, f"cen{b}", tag)
            rows = cen[PASS * b : PASS * (b + 1), :].rearrange("(p t) j -> p t j", t=PACK)
            for h in range(HALVES):
                nc.sync.dma_start(c[:, h, :, :], rows[:, :, HALF * h : HALF * (h + 1)])
            return c

        def prescale(b, t, dst, src, on_scalar=False):
            s = root[:, b, t : t + 1]
            if on_scalar:
                nc.scalar.activation(dst, src, ACT.Copy, scale=s)
            else:
                nc.gpsimd.tensor_scalar(dst, src, s, 0.0, ALU.mult, ALU.add)

        def prescale_pairs(b, dst, src):
            for h in range(HALVES):
                cols = slice(HALF * h, HALF * (h + 1))
                prescale(b, 0, dst[:, 0, cols], src[:, 0, cols])
            for t in range(1, PACK):
                prescale(b, t, dst[:, t, :], src[:, t, :])

        def offset(b, t, h, d):
            acc = psum1.tile([P, HALF], F32, name="acc1")
            m = slice(P * t, P * (t + 1))
            nc.tensor.matmul_mx(
                out=acc[:],
                lhsT=wa_w[b][:, m].bitcast(FP8X4),
                lhsT_scale=wa_s[b][:, m],
                rhs=v_w[h][:].bitcast(FP8X4),
                rhs_scale=v_s[:, HALF * h : HALF * (h + 1)],
                start=True,
                stop=True,
            )
            nc.vector.scalar_tensor_tensor(d, acc[:], root[:, b, t : t + 1], d, ALU.mult, ALU.subtract)

        def offsets_pairs(b, d):
            for t, h in ((0, 0), (0, 1), (1, 0), (1, 1), (2, 0), (3, 0), (2, 1), (3, 1)):
                offset(b, t, h, d[:, t, HALF * h : HALF * (h + 1)])

        def square(hb, d):
            nc.scalar.activation(
                hb.rearrange("p (c i) t -> p c t i", i=4),
                d.rearrange("p t (c i) -> p c t i", i=4),
                ACT.Square,
            )

        def quantise(hb, width, name, tag):
            h_w = slot([P, width], U32, name + "_w", tag)
            h_s = slot([P, width], U8, name + "_s", name + "_s")
            nc.vector.quantize_mx(
                out=h_w[:].bitcast(FP8X4), scales=h_s[:], in_=hb[:].rearrange("p c t -> p (c t)")
            )
            return h_w, h_s

        def second(i, acc, operands):
            for b, (h_w, h_s) in enumerate(operands):
                nc.tensor.matmul_mx(
                    out=acc[:],
                    lhsT=wb_w[:, b, 2 * P * i : 2 * P * (i + 1)].bitcast(FP4X4),
                    lhsT_scale=wb_s[b][:, P * i : P * (i + 1)],
                    rhs=h_w[:].bitcast(FP8X4),
                    rhs_scale=h_s[:],
                    start=(b == 0),
                    stop=(b == BLOCKS - 1),
                )

        def place(h, i, acc, on_vector=False):
            y = ring.tile([P, HALF], F32, name="y", bufs=8)
            if on_vector:
                nc.vector.tensor_scalar(y[:], acc[:], inv_spread[:, i : i + 1], None, ALU.mult)
            else:
                nc.scalar.activation(y[:], acc[:], ACT.Copy, scale=inv_spread[:, i : i + 1])
            cols = slots[:, h * LIST_COLS : (h + 1) * LIST_COLS]
            nc.vector.tensor_tensor(
                pages[i][:].indirect(cols), y[:], wgo_sb[:, HALF * h : HALF * (h + 1)], ALU.mult
            )

        nc.vector.tensor_copy(v_s_picked[:], tab_s[:].indirect(picks[:]))
        nc.scalar.dma_start(v_s[0:MOVED, :].bitcast(I32), v_s_picked[SHIFT : SHIFT + MOVED, :].bitcast(I32))
        nc.vector.tensor_copy(
            wb_w[:].bitcast(U16).rearrange("p a (i m) -> p a i m", i=PACK),
            wb_w_raw[:].bitcast(U16).rearrange("p a (m i) -> p a i m", i=PACK),
        )
        nc.vector.reciprocal(inv_spread[:], spread_sb[:])
        gather(0)
        gather(1)
        prepare_wa(0, [load_wa(0, 0, 2, "wa_raw0a"), load_wa(0, 1, 2, "wa_raw0b")], "slot_e")
        nc.sync.dma_start(slots[:], offs2)
        for q in range(4):
            nc.gpsimd.dma_start(
                wb_s_raw[32 * q : 32 * q + 4 * BLOCKS, :].bitcast(I32),
                wb_scales[:, 4 * q : 4 * q + 4, :].bitcast(I32),
            )
        c0 = load_cen_pairs(0, "slot_b")
        wa1 = [load_wa(1, 0, 2, "slot_c"), load_wa(1, 1, 2, "slot_g")]

        wb_s[0] = slot([P, N], U8, "wb_s0", "slot_e")
        nc.vector.tensor_copy(
            wb_s[0][:].rearrange("p (i m) -> p i m", i=PACK),
            wb_s_raw[:].rearrange("p (m i) -> p i m", i=PACK),
        )
        for a in range(1, BLOCKS):
            nc.sync.dma_start(
                wb_s[a][0:MOVED, :].bitcast(I32), wb_s[0][4 * a : 4 * a + MOVED, :].bitcast(I32)
            )
        c1 = load_cen_pairs(1, "slot_h")
        wa2 = load_wa(2, 0, 1, "slot_c")
        c2 = load_cen_halves(2, "slot_g")

        for t in range(PACK):
            prescale(0, t, c0[:, t, :], c0[:, t, :], on_scalar=(t % 2 == 0))
        offsets_pairs(0, c0)
        prepare_wa(1, wa1, "wa_grouped1")
        hb00 = slot([P, HALF, PACK], BF16, "hb00", "hb00")
        square(hb00[:], c0[:, :, 0:HALF])
        d1 = c1
        prescale_pairs(1, d1, c1)
        q00 = quantise(hb00, HALF, "q00", "q00")
        offsets_pairs(1, d1)
        prepare_wa(2, [wa2], "hb00")
        wgo_sb = slot([P, S], F32, "wgo_sb", "slot_c")
        nc.sync.dma_start(wgo_sb[:], wgo)
        hb10 = slot([P, HALF, PACK], BF16, "hb10", "hb10")
        square(hb10[:], d1[:, :, 0:HALF])
        d2 = [c2[:, h, :, :] for h in range(HALVES)]
        hb2 = [slot([P, HALF, PACK], BF16, f"hb2{h}", f"slot_page{2 + h}") for h in range(HALVES)]
        steps = [(h, t) for h in range(HALVES) for t in range(PACK)]
        for h, t in steps:
            prescale(2, t, d2[h][:, t, :], c2[:, h, t, :])
        for h, t in steps[:PACK]:
            offset(2, t, h, d2[h][:, t, :])
        square(hb2[0][:], d2[0])
        for h, t in steps[PACK:-1]:
            offset(2, t, h, d2[h][:, t, :])
        q10 = quantise(hb10, HALF, "q10", "q10")
        q20 = quantise(hb2[0], HALF, "q20", "q20")
        acc0 = [psum2.tile([P, HALF], F32, name=f"acc2_{i}") for i in range(PACK)]
        for i in range(PACK):
            second(i, acc0[i], (q00, q10, q20))
        offset(2, PACK - 1, 1, d2[1][:, PACK - 1, :])
        for i in range(2):
            nc.vector.memset(pages[i][:], 0.0)
        place(0, 0, acc0[0])
        square(hb2[1][:], d2[1])
        q21 = quantise(hb2[1], HALF, "q21", "q21")
        for i in range(2, PACK):
            pages.append(slot([P, T2], F32, f"page{i}", f"slot_page{i}"))
            nc.gpsimd.memset(pages[i][:], 0.0)
        place(0, 1, acc0[1])
        late = slot([P, HALVES, HALF, PACK], BF16, "hb_late", "slot_g")
        square(late[:, 0, :, :], c0[:, :, HALF:S])
        q01 = quantise(late[:, 0, :, :], HALF, "q01", "q01")
        place(0, 2, acc0[2])
        square(late[:, 1, :, :], d1[:, :, HALF:S])
        q11 = quantise(late[:, 1, :, :], HALF, "q11", "q11")
        place(0, 3, acc0[3])
        acc1 = [psum1.tile([P, HALF], F32, name="acc1") for i in range(PACK)]
        for i in range(PACK):
            second(i, acc1[i], (q01, q11, q21))
        rows = out.rearrange("(p i) t -> p i t", i=PACK)
        for i in range(PACK):
            place(1, i, acc1[i])
            nc.sync.dma_start(rows[:, i, :], pages[i][:])
